import numpy as np
import ml_dtypes


def mxq(x, axis, fmt="e4m3"):
    dtype, down = {"e4m3": (ml_dtypes.float8_e4m3fn, 7), "e5m2": (ml_dtypes.float8_e5m2, 14)}[fmt]
    v = np.moveaxis(np.asarray(x, np.float32).astype(ml_dtypes.bfloat16).astype(np.float64), axis, -1)
    blocks = v.reshape(v.shape[:-1] + (-1, 32))
    amax = np.abs(blocks).max(-1, keepdims=True)
    byte = np.maximum(np.where(amax > 0, np.frexp(amax)[1] - 1 + 127, 0) - down, 1)
    scale = np.exp2(byte - 127.0)
    codes = (blocks / scale).astype(np.float32).astype(dtype).astype(np.float64)
    return np.moveaxis((codes * scale).reshape(v.shape), -1, axis)


WIDE = False


def mx_kscale(k):
    if not WIDE:
        return np.ones(k)
    levels = np.array([10, -10, 5, -5, 0])
    if k % 512:
        return np.exp2(np.random.permutation(np.resize(levels, k // 32))).repeat(32)
    a = np.empty((k // 512, 16))
    for p in range(k // 512):
        a[p, :8] = np.random.permutation(np.resize(levels, 8))
        for g in range(8):
            far = levels[np.abs(levels - a[p, g]) >= 10]
            a[p, g + 8] = far[np.random.randint(len(far))]
    return np.exp2(a.ravel()).repeat(32)


def f64(x):
    return np.asarray(x).astype(np.float64)


def striped(idx):
    return np.tile(idx.reshape(-1, 16).T, (8, 1)).astype(np.uint16)


def unstriped(offs):
    return offs[:16].T.reshape(-1).astype(np.int64)


def striped8(idx):
    return np.concatenate([x.reshape(-1, 16).T for x in idx]).astype(np.uint16)


def runs(offs, k):
    lists = np.stack([offs[16 * r : 16 * r + 16].T.reshape(-1) for r in range(8)]).astype(np.int64)
    return lists[np.arange(k) % 512 // 64]


def pack_weight(w):
    k, n = w.shape
    w = f64(np.asarray(w, np.float32).astype(ml_dtypes.bfloat16)).reshape(k // 32, 32, n)
    amax = np.abs(w).max(1)
    byte = np.clip(np.where(amax > 0, np.frexp(amax)[1] - 1 + 127 - 7, 1), 1, 254)
    scaled = (w * np.exp2(127.0 - byte)[:, None, :]).reshape(k, n).astype(np.float32)
    words = np.ascontiguousarray(scaled.reshape(k // 512, 128, 4, n).transpose(0, 1, 3, 2)).astype(ml_dtypes.float8_e4m3fn).view(np.uint8)
    return words, np.ascontiguousarray(byte.astype(np.uint8).reshape(k // 512, 16, n))


def unpack_weight(words, scales):
    g, p, n, _ = words.shape
    vals = np.ascontiguousarray(words).view(ml_dtypes.float8_e4m3fn).astype(np.float64) * np.repeat(np.exp2(scales.astype(np.float64) - 127.0), 8, axis=1)[..., None]
    return vals.transpose(0, 1, 3, 2).reshape(g * 512, n)


def sigmoid(v):
    return 1.0 / (1.0 + np.exp(-np.maximum(v, -700.0)))

def planes(y):
    n, m = y.shape
    v = y.astype(np.float32).astype(ml_dtypes.bfloat16).astype(np.float64).reshape(n // 32, 32, m)
    top = np.abs(v).max(1)
    byte = np.clip(np.where(top > 0, np.frexp(top)[1] - 1 + 127 - 7, 1), 1, 254)
    codes = (v * np.exp2(127.0 - byte)[:, None, :]).reshape(n, m).astype(np.float32).astype(ml_dtypes.float8_e4m3fn).view(np.uint8)
    words = codes.reshape(n // 512, 128, 4, m).transpose(0, 1, 3, 2)
    return np.ascontiguousarray(words), np.ascontiguousarray(byte.astype(np.uint8).reshape(n // 512, 16, m))


K, T, S, H, C, G = 512, 1024, 512, 512, 512, 2048


def setup_inputs():
    n = np.random.standard_normal
    s = mx_kscale(K)[:, None]
    packed_xT = pack_weight(n((K, T)) * s)
    packed_w1 = pack_weight(n((K, H)) / np.sqrt(K) / s)
    packed_dT = pack_weight(n((K, G)) / s)
    return {
        "x_words": packed_xT[0],
        "x_scales": packed_xT[1],
        "w1_words": packed_w1[0],
        "w1_scales": packed_w1[1],
        "gs": (np.random.uniform(0.5, 1.5, (K, 1)) / s).astype(np.float32),
        "gk": (np.random.uniform(0.5, 1.5, (K, 1)) * s).astype(np.float32),
        "d_words": packed_dT[0],
        "d_scales": packed_dT[1],
        "offs": striped(np.random.permutation(T)[:S]),
        "n1": striped8(np.stack([np.random.permutation(S) for _ in range(8)])),
        "n2": striped8(np.stack([np.random.permutation(S) for _ in range(8)])),
        "n3": striped8(np.stack([np.random.permutation(S) for _ in range(8)])),
        "n4": striped8(np.stack([np.random.permutation(S) for _ in range(8)])),
        "cand": striped(np.random.permutation(T)[:C]),
        "k1": striped8(np.random.randint(0, G, (8, H))),
        "n5": striped(np.random.permutation(S)),
        "n6": striped(np.random.permutation(S)),
    }


def reference(x_words, x_scales, w1_words, w1_scales, gs, gk, d_words, d_scales, offs, n1, n2, n3, n4, cand, k1, n5, n6):
    x_cand = unpack_weight(x_words, x_scales)[:, unstriped(cand)]
    xq = unpack_weight(x_words, x_scales)[:, unstriped(offs)]
    y = unpack_weight(w1_words, w1_scales).T @ xq
    st = y[np.arange(H)[:, None], runs(n1, H)] - y
    z = f64(gs) * (y * (sigmoid(st[np.arange(H)[:, None], runs(n2, H)])))
    a = 0.0625 * ((x_cand.T @ mxq(z, 0, "e4m3")))
    d_k1 = unpack_weight(d_words, d_scales)[np.arange(K)[:, None], runs(k1, K)]
    sq = (y) ** 2
    z2 = f64(gk) * ((y[np.arange(H)[:, None], runs(n4, H)]) / (np.sqrt(sq + sq[np.arange(H)[:, None], runs(n3, H)] + 0.25)))
    b = 0.0625 * ((d_k1.T @ mxq(z2, 0, "e4m3")))
    out_0 = a + (sigmoid(b[:, unstriped(n6)] - b)) * (a[:, unstriped(n5)] - a)
    return (out_0,) + planes(out_0)

@@ -1,0 +1,276 @@
+from contextlib import ExitStack
+
+import concourse.mybir as mybir
+from concourse.masks import make_identity
+
+F32 = mybir.dt.float32
+BF16 = mybir.dt.bfloat16
+I32 = mybir.dt.int32
+U32 = mybir.dt.uint32
+U16 = mybir.dt.uint16
+U8 = mybir.dt.uint8
+FP8X4 = mybir.dt.float8_e4m3fn_x4
+ACT = mybir.ActivationFunctionType
+ALU = mybir.AluOpType
+
+P = 128
+PACK = 4
+T, S, G = 1024, 512, 2048
+HALF = S // 2
+OPT = dict(n3v=4, n1v=3, n6v=2, n5v=3, tail=2, ils=1, warm=0, order=1, wsg=3, ks=7, kw=8, ksg=1, ob=0, oa=0, n3s=1, evb=0, evy=0, gsq=0, eva=2)
+FLOPS = 3 * 2 * 512 * 512 * 512
+
+
+def tile_picked_cdkeypullbhopdrms_none_po_kernel(
+    tc, x_words, x_scales, w1_words, w1_scales, gs, gk, d_words, d_scales,
+    offs, n1, n2, n3, n4, cand, k1, n5, n6, out_0, out_1, out_2,
+):
+    nc = tc.nc
+    with ExitStack() as ctx:
+        keep = ctx.enter_context(tc.tile_pool(name="keep", bufs=1))
+        psum = ctx.enter_context(tc.psum_pool(name="psum", bufs=1))
+
+        def held(shape, dtype, name):
+            return keep.tile(shape, dtype, name=name, align_bytes=64)
+
+        def tiles(shape, dtype, name):
+            return [held(shape, dtype, "%s%d" % (name, t)) for t in range(PACK)]
+
+        def words_of(dram):
+            return dram[0].rearrange("p n t -> p (n t)").bitcast(I32)
+
+        def load_list(dram, name):
+            lst = held([P, S // 16], U16, name)
+            nc.sync.dma_start(lst[:], dram)
+            return lst
+
+        def cols(h):
+            return slice(h * HALF, (h + 1) * HALF)
+
+        def part(lst, h):
+            return lst[:, h * HALF // 16:(h + 1) * HALF // 16]
+
+        def rows4(dst, dram, queues):
+            for q in range(PACK):
+                queues[q].dma_start(dst[32 * q:32 * q + 32, :].bitcast(I32),
+                                    dram[0, 4 * q:4 * q + 4, :].bitcast(I32).partition_broadcast(8))
+
+        xs = held([P, T], U8, "xs")
+        ws = held([P, S], U8, "ws")
+        ds = held([P, G], U8, "ds")
+        key_s = held([P, S], U8, "key_s")
+        xw = held([P, T], U32, "xw")
+        ww = held([P, S], U32, "ww")
+        dw = held([P, G], U32, "dw")
+        gs_t = held([P, PACK], F32, "gs_t")
+        gk_t = held([P, PACK], F32, "gk_t")
+        nc.vector.memset(key_s[:].bitcast(I32), 0)
+        if OPT["warm"]:
+            warm = held([P, 2], F32, "warm")
+            nc.vector.memset(warm[:, 0:1], 1.0)
+            nc.scalar.activation(warm[:, 1:2], warm[:, 0:1], ACT.Abs_reciprocal_sqrt)
+
+        offs_l = load_list(offs, "offs_l")
+        rows4(xs, x_scales, [nc.sync] * 4)
+        nc.sync.dma_start(xw[:].bitcast(I32), words_of(x_words))
+        nc.sync.dma_start(ww[:].bitcast(I32), words_of(w1_words))
+        rows4(ws, w1_scales, [nc.sync] * (4 - OPT["wsg"]) + [nc.gpsimd] * OPT["wsg"])
+        n4_l = load_list(n4, "n4_l")
+        cand_l = load_list(cand, "cand_l")
+        n3_l = load_list(n3, "n3_l")
+        k1_l = load_list(k1, "k1_l")
+        nc.vector.memset(ds[:].bitcast(I32), 0)
+        for e in range(2):
+            nc.sync.dma_start(ds[e:P:16, :].bitcast(I32), d_scales[0, e:16:2, :].bitcast(I32))
+        nc.sync.dma_start(dw[:].bitcast(I32), words_of(d_words))
+        n1_l = load_list(n1, "n1_l")
+        nc.sync.dma_start(gk_t[:], gk.rearrange("(p t) o -> p (t o)", t=PACK))
+        nc.sync.dma_start(gs_t[:], gs.rearrange("(p t) o -> p (t o)", t=PACK))
+        n2_l = load_list(n2, "n2_l")
+        n6_l = load_list(n6, "n6_l")
+        n5_l = load_list(n5, "n5_l")
+
+        def deal(engine_copy, src, dtype, name):
+            dst = held([P, S], dtype, name)
+            d, s = dst[:], src[:]
+            engine_copy(d.rearrange("p (t m) -> p t m", t=PACK), s.rearrange("p (m t) -> p t m", t=PACK))
+            return dst
+
+        def vcopy(o, i):
+            nc.vector.tensor_copy(o, i)
+
+        def pick(window, lst, dtype, name):
+            dst = held([P, S], dtype, name)
+            nc.vector.tensor_copy(dst[:], window[:].indirect(lst[:]))
+            return dst
+
+        def product(bank, t, lw, ls, rw, rs):
+            m = slice(t * P, (t + 1) * P)
+            nc.tensor.matmul_mx(out=bank[:], lhsT=lw[:, m].bitcast(FP8X4), lhsT_scale=ls[:, m],
+                                rhs=rw[:].bitcast(FP8X4), rhs_scale=rs[:], start=True, stop=True)
+
+        def weave(copy, woven, planes):
+            copy(woven.rearrange("p (c i) t -> p c t i", i=4), planes.rearrange("p t (c i) -> p c t i", i=4))
+
+        def quantise(planes, name):
+            woven = held([P, S, PACK], BF16, name + "_woven")
+            weave(vcopy, woven[:], planes[:])
+            qw = held([P, S], U32, name + "_words")
+            qs = held([P, S], U8, name + "_scales")
+            nc.vector.quantize_mx(out=qw[:].bitcast(FP8X4), scales=qs[:], in_=woven[:].rearrange("p c t -> p (c t)"))
+            return qw, qs
+
+        ident = held([P, P], F32, "ident")
+        make_identity(nc, ident[:])
+
+        def turned_sum(name, parts):
+            bank = psum.tile([P, S], F32, name=name)
+            steps = [(x, c) for x in parts for c in range(PACK)]
+            for i, (x, c) in enumerate(steps):
+                blk = slice(c * P, (c + 1) * P)
+                nc.tensor.matmul(bank[:, blk], x[:, blk], ident[:], start=(i == 0), stop=(i == len(steps) - 1), is_transpose=True)
+            return bank
+
+        LO, HI = slice(0, S), slice(S, 2 * S)
+        xq_s = pick(xs, offs_l, U8, "xq_s")
+        xq_w = pick(xw, offs_l, U32, "xq_w")
+        w_w = deal(nc.scalar.copy, ww, U32, "w_w")
+        w_s = deal(vcopy, ws, U8, "w_s")
+
+        yw = tiles([P, 2 * S], F32, "y")
+        sqw = tiles([P, 2 * S], F32, "sq")
+        stw = tiles([P, 2 * S], F32, "st")
+        bw = tiles([P, 2 * S], F32, "b")
+        aw = tiles([P, 2 * S], F32, "a")
+        y4 = tiles([P, S], F32, "y4")
+        y4 = [y4[t][:] if t < OPT["n1v"] else stw[t][:, LO] for t in range(PACK)]
+        tmp = [bw[t][:, HI] for t in range(PACK)]
+        for t in range(PACK):
+            nc.vector.memset(sqw[t][:, HI], 0.0)
+            nc.vector.memset(yw[t][:, HI], 0.0)
+        banks = [psum.tile([P, S], F32, name="bank%d" % t) for t in range(PACK)]
+        for t in range(PACK):
+            product(banks[t], t, w_w, w_s, xq_w, xq_s)
+            if not OPT["gsq"]:
+                nc.scalar.activation(sqw[t][:, LO], banks[t][:], ACT.Square)
+        for t in range(PACK):
+            if t < OPT["evy"]:
+                nc.vector.tensor_copy(yw[t][:, LO], banks[t][:])
+            else:
+                nc.scalar.copy(yw[t][:, LO], banks[t][:])
+            if OPT["gsq"]:
+                nc.gpsimd.tensor_tensor(sqw[t][:, LO], yw[t][:, LO], yw[t][:, LO], ALU.mult)
+            if not OPT["gsq"]:
+                nc.sync.dma_start(stw[t][:, HI], yw[t][:, LO])
+        if OPT["gsq"]:
+            for t in range(PACK):
+                nc.sync.dma_start(stw[t][:, HI], yw[t][:, LO])
+
+        def pick2(window, lst, dtype, name, tag):
+            dst = keep.tile([P, S], dtype, name=name, tag=tag, align_bytes=64)
+            nc.vector.tensor_copy(dst[:], window[:].indirect(lst[:]))
+            return dst
+
+        def keys():
+            dk_s = deal(vcopy, pick2(ds, k1_l, U8, "dk_s", "sq%d" % OPT["ks"]), U8, "dk_sd")
+            for r in range(PACK):
+                src = 16 * (r // 2) + r % 2
+                (nc.gpsimd if OPT["ksg"] else nc.sync).dma_start(key_s[r:P:32, :].bitcast(I32), dk_s[src:P:32, :].bitcast(I32))
+            key_w = deal(vcopy, pick2(dw, k1_l, U32, "dk_w", "sq%d" % OPT["kw"]), U32, "key_w")
+            return key_w
+
+        def cands():
+            return (deal(vcopy, pick(xw, cand_l, U32, "xc_w"), U32, "cand_w"),
+                    deal(vcopy, pick(xs, cand_l, U8, "xc_s"), U8, "cand_s"))
+
+        z2 = held([P, PACK, S], BF16, "z2")
+        den = held([P, PACK, S], F32, "den")
+        rs = held([P, PACK, S], F32, "rs")
+        for t in range(PACK):
+            if (OPT["n3s"] >> t) & 1:
+                nc.scalar.activation(tmp[t], sqw[t][:].indirect(n3_l[:]), ACT.Copy)
+            else:
+                nc.vector.tensor_copy(tmp[t], sqw[t][:].indirect(n3_l[:]))
+        for t in range(PACK):
+            nc.scalar.activation(y4[t], yw[t][:].indirect(n4_l[:]), ACT.Copy)
+        rsr = []
+        for t in range(PACK):
+            bank = turned_sum("bank%d" % ((4 + t) % 8), [sqw[t][:, LO], tmp[t]])
+            nc.scalar.activation(rs[:, t, :], bank[:], ACT.Abs_reciprocal_sqrt, bias=0.25)
+        for t in range(PACK):
+            rsr.append(turned_sum("bank%d" % t, [rs[:, t, :]])[:])
+        def sts(ts):
+            for t in ts:
+                nc.vector.tensor_tensor(stw[t][:, LO], yw[t][:].indirect(n1_l[:]), stw[t][:, HI], ALU.subtract)
+        sts(range(OPT["n1v"]))
+        for t in range(PACK):
+            nc.vector.scalar_tensor_tensor(z2[:, t, :], y4[t], gk_t[:, t:t + 1], rsr[t], ALU.mult, ALU.mult)
+        key_w = keys()
+        z2_w, z2_s = quantise(z2, "z2q")
+        sts(range(OPT["n1v"], PACK))
+        cand_w, cand_s = cands()
+
+        z = held([P, PACK, S], BF16, "z")
+        for t in range(PACK):
+            sg = den[:, t, :]
+            nc.scalar.activation(sg, stw[t][:].indirect(n2_l[:]), ACT.Sigmoid)
+            nc.vector.scalar_tensor_tensor(z[:, t, :], yw[t][:, LO], gs_t[:, t:t + 1], sg, ALU.mult, ALU.mult)
+        z_w, z_s = quantise(z, "zq")
+
+        b6 = tiles([P, S], F32, "b6")
+        db = [aw[t][:, HI] for t in range(PACK)]
+        gate = tiles([P, S], F32, "gate")
+        a5 = tiles([P, S], F32, "a5")
+        da = tiles([P, S], F32, "da")
+        pull = tiles([P, S], F32, "pull")
+        res = held([P, PACK, S], F32, "res")
+        out_rows = out_0.rearrange("(p t) j -> p t j", t=PACK)
+        def bpart(t):
+            bank = psum.tile([P, S], F32, name="bank%d" % t)
+            product(bank, t, key_w, key_s, z2_w, z2_s)
+            if t < OPT["evb"]:
+                nc.vector.tensor_copy(bw[t][:, LO], bank[:])
+            else:
+                nc.scalar.copy(bw[t][:, LO], bank[:])
+            if t < OPT["n6v"]:
+                nc.sync.dma_start(b6[t][:], bw[t][:, LO])
+                nc.vector.tensor_tensor(db[t], bw[t][:].indirect(n6_l[:]), b6[t][:], ALU.subtract)
+                nc.scalar.activation(gate[t][:], db[t], ACT.Sigmoid, scale=0.0625)
+            else:
+                nc.scalar.activation(db[t], bw[t][:].indirect(n6_l[:]), ACT.Copy, scale=-1.0)
+                bank = turned_sum("bank%d" % (4 + t % 2), [bw[t][:, LO], db[t]])
+                nc.scalar.activation(gate[t][:], bank[:], ACT.Sigmoid, scale=-0.0625)
+        def apart(t):
+            bank = psum.tile([P, S], F32, name="bank%d" % ((6 + t) % 8))
+            product(bank, t, cand_w, cand_s, z_w, z_s)
+            a = aw[t][:, LO]
+            if t < OPT["eva"]:
+                nc.vector.tensor_scalar(a, bank[:], 0.0625, None, ALU.mult)
+            else:
+                nc.scalar.activation(a, bank[:], ACT.Copy, scale=0.0625)
+            if t >= OPT["n6v"]:
+                nc.scalar.activation(a5[t][:], aw[t][:].indirect(n5_l[:]), ACT.Copy, scale=-1.0)
+                bank = turned_sum("bank%d" % (2 + t % 2), [a, a5[t][:]])
+                nc.vector.tensor_tensor(pull[t][:], bank[:], gate[t][:], ALU.mult)
+                bank = turned_sum("bank%d" % (4 + t % 2), [pull[t][:]])
+                nc.vector.tensor_tensor(res[:, t, :], a, bank[:], ALU.subtract)
+            else:
+                nc.vector.tensor_tensor(a5[t][:], aw[t][:].indirect(n5_l[:]), gate[t][:], ALU.mult)
+                nc.vector.scalar_tensor_tensor(da[t][:], gate[t][:], -1.0, a, ALU.add, ALU.mult)
+                nc.vector.tensor_tensor(res[:, t, :], a5[t][:], da[t][:], ALU.subtract)
+            nc.sync.dma_start(out_rows[:, t, :], res[:, t, :])
+        for c in ["b0 a0 b1 a1 b2 a2 b3 a3", "b0 b1 b2 b3 a0 a2 a1 a3", "b0 b1 b2 b3 a2 a0 a3 a1", "b0 b1 b2 a0 a2 b3 a1 a3", "b0 b2 a0 a2 b1 b3 a3 a1", "b2 b0 a2 a0 b3 b1 a3 a1", "b0 b1 b2 b3 a2 a3 a0 a1"][OPT["order"]].split():
+            (bpart if c.startswith("b") else apart)(int(c[1]))
+        woven = held([P, S, PACK], BF16, "o_woven")
+        o_w = held([P, S], U32, "o_w")
+        o_s = held([P, S], U8, "o_s")
+        n = OPT["tail"]
+        for h in range(n):
+            c = slice(h * S // n, (h + 1) * S // n)
+            weave(nc.scalar.copy if h >= n - OPT["ils"] else vcopy, woven[:, c, :], res[:, :, c])
+        for h in range(n):
+            c = slice(h * S // n, (h + 1) * S // n)
+            nc.vector.quantize_mx(out=o_w[:, c].bitcast(FP8X4), scales=o_s[:, c], in_=woven[:, c, :].rearrange("p c t -> p (c t)"))
+            nc.sync.dma_start(words_of(out_1)[:, c], o_w[:, c].bitcast(I32))
+        for r in range(PACK):
+            nc.scalar.dma_start(out_2[0, r:16:4, :].bitcast(I32), o_s[r:P:32, :].bitcast(I32))

@@ -15,10 +15,20 @@ ALU = mybir.AluOpType
 
 P = 128
 PACK = 4
+QUAD = 32
+GROUP = 16
+BLOCKS = 16
+LINE = 16
 T, S, G = 1024, 512, 2048
-HALF = S // 2
-OPT = dict(n3v=4, n1v=3, n6v=2, n5v=3, tail=2, ils=1, warm=0, order=1, wsg=3, ks=7, kw=8, ksg=1, ob=0, oa=0, n3s=1, evb=0, evy=0, gsq=0, eva=2)
-FLOPS = 3 * 2 * 512 * 512 * 512
+SCORE_SCALE = 0.0625
+FLOPS = 3 * 2 * S * S * S
+
+PLANES = range(PACK)
+ON_VECTOR = range(0, PACK // 2)
+ON_SCALAR = range(PACK // 2, PACK)
+EARLY_ST = range(0, PACK - 1)
+LAST = PACK - 1
+LO, HI = slice(0, S), slice(S, 2 * S)
 
 
 def tile_picked_cdkeypullbhopdrms_none_po_kernel(
@@ -30,59 +40,86 @@ def tile_picked_cdkeypullbhopdrms_none_po_kernel(
         keep = ctx.enter_context(tc.tile_pool(name="keep", bufs=1))
         psum = ctx.enter_context(tc.psum_pool(name="psum", bufs=1))
 
-        def held(shape, dtype, name):
-            return keep.tile(shape, dtype, name=name, align_bytes=64)
+        def held(shape, dtype, name, tag=""):
+            return keep.tile(shape, dtype, name=name, tag=tag, align_bytes=64)
 
-        def tiles(shape, dtype, name):
-            return [held(shape, dtype, "%s%d" % (name, t)) for t in range(PACK)]
+        def per_plane(shape, name, planes=PLANES):
+            return {t: held(shape, F32, "%s%d" % (name, t)) for t in planes}
+
+        def bank(number):
+            return psum.tile([P, S], F32, name="bank%d" % number)
 
         def words_of(dram):
             return dram[0].rearrange("p n t -> p (n t)").bitcast(I32)
 
         def load_list(dram, name):
-            lst = held([P, S // 16], U16, name)
-            nc.sync.dma_start(lst[:], dram)
-            return lst
+            entries = held([P, S // GROUP], U16, name)
+            nc.sync.dma_start(entries[:], dram)
+            return entries
 
-        def cols(h):
-            return slice(h * HALF, (h + 1) * HALF)
+        def load_scale_rows(dst, dram):
+            for r in range(PACK):
+                nc.sync.dma_start(dst[r:P:QUAD, :].bitcast(I32), dram[0, r:BLOCKS:PACK, :].bitcast(I32))
 
-        def part(lst, h):
-            return lst[:, h * HALF // 16:(h + 1) * HALF // 16]
+        def pick(window, entries, dtype, name):
+            picked = held([P, S], dtype, name)
+            nc.vector.tensor_copy(picked[:], window[:].indirect(entries[:]))
+            return picked
 
-        def rows4(dst, dram, queues):
-            for q in range(PACK):
-                queues[q].dma_start(dst[32 * q:32 * q + 32, :].bitcast(I32),
-                                    dram[0, 4 * q:4 * q + 4, :].bitcast(I32).partition_broadcast(8))
+        def deal(copy, src, dtype, name):
+            dealt = held([P, S], dtype, name)
+            run = LINE // PACK if dtype == U32 else LINE
+            copy(dealt[:].rearrange("p (t m i) -> p m t i", t=PACK, i=run),
+                 src[:].rearrange("p (m i t) -> p m t i", t=PACK, i=run))
+            return dealt
 
-        xs = held([P, T], U8, "xs")
-        ws = held([P, S], U8, "ws")
-        ds = held([P, G], U8, "ds")
+        def product(dst, t, left_words, left_scales, right_words, right_scales):
+            rows = slice(t * P, (t + 1) * P)
+            nc.tensor.matmul_mx(out=dst[:], lhsT=left_words[:, rows].bitcast(FP8X4), lhsT_scale=left_scales[:, rows],
+                                rhs=right_words[:].bitcast(FP8X4), rhs_scale=right_scales[:], start=True, stop=True)
+
+        def weave(copy, woven, planes):
+            copy(woven.rearrange("p (c i) t -> p c t i", i=PACK), planes.rearrange("p t (c i) -> p c t i", i=PACK))
+
+        def quantise(planes, name):
+            woven = held([P, S, PACK], BF16, name + "_woven")
+            weave(nc.vector.tensor_copy, woven[:], planes[:])
+            words = held([P, S], U32, name + "_words")
+            scales = held([P, S], U8, name + "_scales")
+            nc.vector.quantize_mx(out=words[:].bitcast(FP8X4), scales=scales[:],
+                                  in_=woven[:].rearrange("p j t -> p (j t)"))
+            return words, scales
+
+        x_s = held([P, T], U8, "x_s")
+        w_s = held([P, S], U8, "w_s")
+        d_s = held([P, G], U8, "d_s")
         key_s = held([P, S], U8, "key_s")
-        xw = held([P, T], U32, "xw")
-        ww = held([P, S], U32, "ww")
-        dw = held([P, G], U32, "dw")
+        x_w = held([P, T], U32, "x_w")
+        w_w = held([P, S], U32, "w_w")
+        d_w = held([P, G], U32, "d_w")
         gs_t = held([P, PACK], F32, "gs_t")
         gk_t = held([P, PACK], F32, "gk_t")
+        nc.gpsimd.memset(x_s[:].bitcast(I32), 0)
+        nc.gpsimd.memset(w_s[:].bitcast(I32), 0)
+        nc.gpsimd.memset(d_s[:].bitcast(I32), 0)
         nc.vector.memset(key_s[:].bitcast(I32), 0)
-        if OPT["warm"]:
-            warm = held([P, 2], F32, "warm")
-            nc.vector.memset(warm[:, 0:1], 1.0)
-            nc.scalar.activation(warm[:, 1:2], warm[:, 0:1], ACT.Abs_reciprocal_sqrt)
+
+        warm = held([P, 2], F32, "warm")
+        nc.vector.memset(warm[:, 0:1], 1.0)
+        nc.scalar.activation(warm[:, 1:2], warm[:, 0:1], ACT.Abs_reciprocal_sqrt)
 
         offs_l = load_list(offs, "offs_l")
-        rows4(xs, x_scales, [nc.sync] * 4)
-        nc.sync.dma_start(xw[:].bitcast(I32), words_of(x_words))
-        nc.sync.dma_start(ww[:].bitcast(I32), words_of(w1_words))
-        rows4(ws, w1_scales, [nc.sync] * (4 - OPT["wsg"]) + [nc.gpsimd] * OPT["wsg"])
+        load_scale_rows(x_s, x_scales)
+        nc.sync.dma_start(x_w[:].bitcast(I32), words_of(x_words))
+        nc.sync.dma_start(w_w[:].bitcast(I32), words_of(w1_words))
+        load_scale_rows(w_s, w1_scales)
         n4_l = load_list(n4, "n4_l")
         cand_l = load_list(cand, "cand_l")
         n3_l = load_list(n3, "n3_l")
         k1_l = load_list(k1, "k1_l")
-        nc.vector.memset(ds[:].bitcast(I32), 0)
         for e in range(2):
-            nc.sync.dma_start(ds[e:P:16, :].bitcast(I32), d_scales[0, e:16:2, :].bitcast(I32))
-        nc.sync.dma_start(dw[:].bitcast(I32), words_of(d_words))
+            nc.sync.dma_start(d_s[e:P:GROUP, :].bitcast(I32), d_scales[0, e:BLOCKS:2, :].bitcast(I32))
+        nc.sync.dma_start(d_w[:].bitcast(I32), words_of(d_words))
         n1_l = load_list(n1, "n1_l")
         nc.sync.dma_start(gk_t[:], gk.rearrange("(p t) o -> p (t o)", t=PACK))
         nc.sync.dma_start(gs_t[:], gs.rearrange("(p t) o -> p (t o)", t=PACK))
@@ -90,187 +127,138 @@ def tile_picked_cdkeypullbhopdrms_none_po_kernel(
         n6_l = load_list(n6, "n6_l")
         n5_l = load_list(n5, "n5_l")
 
-        def deal(engine_copy, src, dtype, name):
-            dst = held([P, S], dtype, name)
-            d, s = dst[:], src[:]
-            engine_copy(d.rearrange("p (t m) -> p t m", t=PACK), s.rearrange("p (m t) -> p t m", t=PACK))
+        identity = held([P, P], F32, "identity")
+
+        def turned_sum(dst, terms):
+            steps = [(term, c) for term in terms for c in range(S // P)]
+            for i, (term, c) in enumerate(steps):
+                block = slice(c * P, (c + 1) * P)
+                nc.tensor.matmul(dst[:, block], term[:, block], identity[:],
+                                 start=(i == 0), stop=(i == len(steps) - 1), is_transpose=True)
             return dst
 
-        def vcopy(o, i):
-            nc.vector.tensor_copy(o, i)
+        xq_s = pick(x_s, offs_l, U8, "xq_s")
+        xq_w = pick(x_w, offs_l, U32, "xq_w")
+        wd_w = deal(nc.scalar.copy, w_w, U32, "wd_w")
+        wd_s = deal(nc.vector.tensor_copy, w_s, U8, "wd_s")
 
-        def pick(window, lst, dtype, name):
-            dst = held([P, S], dtype, name)
-            nc.vector.tensor_copy(dst[:], window[:].indirect(lst[:]))
-            return dst
+        y_win = per_plane([P, 2 * S], "y")
+        sq_win = per_plane([P, 2 * S], "sq")
+        st_win = per_plane([P, 2 * S], "st")
+        b_win = per_plane([P, 2 * S], "b")
+        a_win = per_plane([P, 2 * S], "a")
+        y_n4 = {t: b_win[t][:, HI] if t in EARLY_ST else st_win[t][:, LO] for t in PLANES}
+        sq_n3 = {t: st_win[t][:, HI] if t in EARLY_ST else b_win[t][:, HI] for t in PLANES}
+        y_early = held([P, len(EARLY_ST), S], F32, "y_early", tag="planes")
+        y_copy = {t: y_early[:, t, :] if t in EARLY_ST else st_win[t][:, HI] for t in PLANES}
+        for t in PLANES:
+            nc.vector.memset(sq_win[t][:, HI], 0.0)
+            nc.gpsimd.memset(y_win[t][:, HI], 0.0)
+        make_identity(nc, identity[:])
 
-        def product(bank, t, lw, ls, rw, rs):
-            m = slice(t * P, (t + 1) * P)
-            nc.tensor.matmul_mx(out=bank[:], lhsT=lw[:, m].bitcast(FP8X4), lhsT_scale=ls[:, m],
-                                rhs=rw[:].bitcast(FP8X4), rhs_scale=rs[:], start=True, stop=True)
+        y_banks = [bank(t) for t in PLANES]
+        for t in PLANES:
+            product(y_banks[t], t, wd_w, wd_s, xq_w, xq_s)
+        for t in PLANES:
+            nc.scalar.copy(y_win[t][:, LO], y_banks[t][:])
+            nc.gpsimd.tensor_tensor(sq_win[t][:, LO], y_win[t][:, LO], y_win[t][:, LO], ALU.mult)
+        for t in PLANES:
+            nc.sync.dma_start(y_copy[t], y_win[t][:, LO])
 
-        def weave(copy, woven, planes):
-            copy(woven.rearrange("p (c i) t -> p c t i", i=4), planes.rearrange("p t (c i) -> p c t i", i=4))
+        z2 = held([P, PACK, S], BF16, "z2", tag="planes")
+        root_turned = held([P, PACK, S], F32, "root_turned", tag="scalar_out")
+        for t in ON_VECTOR:
+            nc.vector.tensor_copy(sq_n3[t], sq_win[t][:].indirect(n3_l[:]))
+        for t in ON_SCALAR:
+            nc.scalar.activation(sq_n3[t], sq_win[t][:].indirect(n3_l[:]), ACT.Copy)
+        for t in PLANES:
+            nc.scalar.activation(y_n4[t], y_win[t][:].indirect(n4_l[:]), ACT.Copy)
+        for t in PLANES:
+            total = turned_sum(bank(PACK + t), [sq_win[t][:, LO], sq_n3[t]])
+            nc.scalar.activation(root_turned[:, t, :], total[:], ACT.Abs_reciprocal_sqrt, bias=0.25)
+        inverse_root = [turned_sum(bank(t), [root_turned[:, t, :]]) for t in PLANES]
 
-        def quantise(planes, name):
-            woven = held([P, S, PACK], BF16, name + "_woven")
-            weave(vcopy, woven[:], planes[:])
-            qw = held([P, S], U32, name + "_words")
-            qs = held([P, S], U8, name + "_scales")
-            nc.vector.quantize_mx(out=qw[:].bitcast(FP8X4), scales=qs[:], in_=woven[:].rearrange("p c t -> p (c t)"))
-            return qw, qs
+        def form_st(t):
+            nc.vector.tensor_tensor(st_win[t][:, LO], y_win[t][:].indirect(n1_l[:]), y_copy[t], ALU.subtract)
 
-        ident = held([P, P], F32, "ident")
-        make_identity(nc, ident[:])
+        for t in EARLY_ST:
+            form_st(t)
+        for t in PLANES:
+            nc.vector.scalar_tensor_tensor(z2[:, t, :], y_n4[t], gk_t[:, t:t + 1], inverse_root[t][:], ALU.mult, ALU.mult)
 
-        def turned_sum(name, parts):
-            bank = psum.tile([P, S], F32, name=name)
-            steps = [(x, c) for x in parts for c in range(PACK)]
-            for i, (x, c) in enumerate(steps):
-                blk = slice(c * P, (c + 1) * P)
-                nc.tensor.matmul(bank[:, blk], x[:, blk], ident[:], start=(i == 0), stop=(i == len(steps) - 1), is_transpose=True)
-            return bank
-
-        LO, HI = slice(0, S), slice(S, 2 * S)
-        xq_s = pick(xs, offs_l, U8, "xq_s")
-        xq_w = pick(xw, offs_l, U32, "xq_w")
-        w_w = deal(nc.scalar.copy, ww, U32, "w_w")
-        w_s = deal(vcopy, ws, U8, "w_s")
-
-        yw = tiles([P, 2 * S], F32, "y")
-        sqw = tiles([P, 2 * S], F32, "sq")
-        stw = tiles([P, 2 * S], F32, "st")
-        bw = tiles([P, 2 * S], F32, "b")
-        aw = tiles([P, 2 * S], F32, "a")
-        y4 = tiles([P, S], F32, "y4")
-        y4 = [y4[t][:] if t < OPT["n1v"] else stw[t][:, LO] for t in range(PACK)]
-        tmp = [bw[t][:, HI] for t in range(PACK)]
-        for t in range(PACK):
-            nc.vector.memset(sqw[t][:, HI], 0.0)
-            nc.vector.memset(yw[t][:, HI], 0.0)
-        banks = [psum.tile([P, S], F32, name="bank%d" % t) for t in range(PACK)]
-        for t in range(PACK):
-            product(banks[t], t, w_w, w_s, xq_w, xq_s)
-            if not OPT["gsq"]:
-                nc.scalar.activation(sqw[t][:, LO], banks[t][:], ACT.Square)
-        for t in range(PACK):
-            if t < OPT["evy"]:
-                nc.vector.tensor_copy(yw[t][:, LO], banks[t][:])
-            else:
-                nc.scalar.copy(yw[t][:, LO], banks[t][:])
-            if OPT["gsq"]:
-                nc.gpsimd.tensor_tensor(sqw[t][:, LO], yw[t][:, LO], yw[t][:, LO], ALU.mult)
-            if not OPT["gsq"]:
-                nc.sync.dma_start(stw[t][:, HI], yw[t][:, LO])
-        if OPT["gsq"]:
-            for t in range(PACK):
-                nc.sync.dma_start(stw[t][:, HI], yw[t][:, LO])
-
-        def pick2(window, lst, dtype, name, tag):
-            dst = keep.tile([P, S], dtype, name=name, tag=tag, align_bytes=64)
-            nc.vector.tensor_copy(dst[:], window[:].indirect(lst[:]))
-            return dst
-
-        def keys():
-            dk_s = deal(vcopy, pick2(ds, k1_l, U8, "dk_s", "sq%d" % OPT["ks"]), U8, "dk_sd")
-            for r in range(PACK):
-                src = 16 * (r // 2) + r % 2
-                (nc.gpsimd if OPT["ksg"] else nc.sync).dma_start(key_s[r:P:32, :].bitcast(I32), dk_s[src:P:32, :].bitcast(I32))
-            key_w = deal(vcopy, pick2(dw, k1_l, U32, "dk_w", "sq%d" % OPT["kw"]), U32, "key_w")
-            return key_w
-
-        def cands():
-            return (deal(vcopy, pick(xw, cand_l, U32, "xc_w"), U32, "cand_w"),
-                    deal(vcopy, pick(xs, cand_l, U8, "xc_s"), U8, "cand_s"))
-
-        z2 = held([P, PACK, S], BF16, "z2")
-        den = held([P, PACK, S], F32, "den")
-        rs = held([P, PACK, S], F32, "rs")
-        for t in range(PACK):
-            if (OPT["n3s"] >> t) & 1:
-                nc.scalar.activation(tmp[t], sqw[t][:].indirect(n3_l[:]), ACT.Copy)
-            else:
-                nc.vector.tensor_copy(tmp[t], sqw[t][:].indirect(n3_l[:]))
-        for t in range(PACK):
-            nc.scalar.activation(y4[t], yw[t][:].indirect(n4_l[:]), ACT.Copy)
-        rsr = []
-        for t in range(PACK):
-            bank = turned_sum("bank%d" % ((4 + t) % 8), [sqw[t][:, LO], tmp[t]])
-            nc.scalar.activation(rs[:, t, :], bank[:], ACT.Abs_reciprocal_sqrt, bias=0.25)
-        for t in range(PACK):
-            rsr.append(turned_sum("bank%d" % t, [rs[:, t, :]])[:])
-        def sts(ts):
-            for t in ts:
-                nc.vector.tensor_tensor(stw[t][:, LO], yw[t][:].indirect(n1_l[:]), stw[t][:, HI], ALU.subtract)
-        sts(range(OPT["n1v"]))
-        for t in range(PACK):
-            nc.vector.scalar_tensor_tensor(z2[:, t, :], y4[t], gk_t[:, t:t + 1], rsr[t], ALU.mult, ALU.mult)
-        key_w = keys()
-        z2_w, z2_s = quantise(z2, "z2q")
-        sts(range(OPT["n1v"], PACK))
-        cand_w, cand_s = cands()
-
-        z = held([P, PACK, S], BF16, "z")
-        for t in range(PACK):
-            sg = den[:, t, :]
-            nc.scalar.activation(sg, stw[t][:].indirect(n2_l[:]), ACT.Sigmoid)
-            nc.vector.scalar_tensor_tensor(z[:, t, :], yw[t][:, LO], gs_t[:, t:t + 1], sg, ALU.mult, ALU.mult)
-        z_w, z_s = quantise(z, "zq")
-
-        b6 = tiles([P, S], F32, "b6")
-        db = [aw[t][:, HI] for t in range(PACK)]
-        gate = tiles([P, S], F32, "gate")
-        a5 = tiles([P, S], F32, "a5")
-        da = tiles([P, S], F32, "da")
-        pull = tiles([P, S], F32, "pull")
-        res = held([P, PACK, S], F32, "res")
-        out_rows = out_0.rearrange("(p t) j -> p t j", t=PACK)
-        def bpart(t):
-            bank = psum.tile([P, S], F32, name="bank%d" % t)
-            product(bank, t, key_w, key_s, z2_w, z2_s)
-            if t < OPT["evb"]:
-                nc.vector.tensor_copy(bw[t][:, LO], bank[:])
-            else:
-                nc.scalar.copy(bw[t][:, LO], bank[:])
-            if t < OPT["n6v"]:
-                nc.sync.dma_start(b6[t][:], bw[t][:, LO])
-                nc.vector.tensor_tensor(db[t], bw[t][:].indirect(n6_l[:]), b6[t][:], ALU.subtract)
-                nc.scalar.activation(gate[t][:], db[t], ACT.Sigmoid, scale=0.0625)
-            else:
-                nc.scalar.activation(db[t], bw[t][:].indirect(n6_l[:]), ACT.Copy, scale=-1.0)
-                bank = turned_sum("bank%d" % (4 + t % 2), [bw[t][:, LO], db[t]])
-                nc.scalar.activation(gate[t][:], bank[:], ACT.Sigmoid, scale=-0.0625)
-        def apart(t):
-            bank = psum.tile([P, S], F32, name="bank%d" % ((6 + t) % 8))
-            product(bank, t, cand_w, cand_s, z_w, z_s)
-            a = aw[t][:, LO]
-            if t < OPT["eva"]:
-                nc.vector.tensor_scalar(a, bank[:], 0.0625, None, ALU.mult)
-            else:
-                nc.scalar.activation(a, bank[:], ACT.Copy, scale=0.0625)
-            if t >= OPT["n6v"]:
-                nc.scalar.activation(a5[t][:], aw[t][:].indirect(n5_l[:]), ACT.Copy, scale=-1.0)
-                bank = turned_sum("bank%d" % (2 + t % 2), [a, a5[t][:]])
-                nc.vector.tensor_tensor(pull[t][:], bank[:], gate[t][:], ALU.mult)
-                bank = turned_sum("bank%d" % (4 + t % 2), [pull[t][:]])
-                nc.vector.tensor_tensor(res[:, t, :], a, bank[:], ALU.subtract)
-            else:
-                nc.vector.tensor_tensor(a5[t][:], aw[t][:].indirect(n5_l[:]), gate[t][:], ALU.mult)
-                nc.vector.scalar_tensor_tensor(da[t][:], gate[t][:], -1.0, a, ALU.add, ALU.mult)
-                nc.vector.tensor_tensor(res[:, t, :], a5[t][:], da[t][:], ALU.subtract)
-            nc.sync.dma_start(out_rows[:, t, :], res[:, t, :])
-        for c in ["b0 a0 b1 a1 b2 a2 b3 a3", "b0 b1 b2 b3 a0 a2 a1 a3", "b0 b1 b2 b3 a2 a0 a3 a1", "b0 b1 b2 a0 a2 b3 a1 a3", "b0 b2 a0 a2 b1 b3 a3 a1", "b2 b0 a2 a0 b3 b1 a3 a1", "b0 b1 b2 b3 a2 a3 a0 a1"][OPT["order"]].split():
-            (bpart if c.startswith("b") else apart)(int(c[1]))
-        woven = held([P, S, PACK], BF16, "o_woven")
-        o_w = held([P, S], U32, "o_w")
-        o_s = held([P, S], U8, "o_s")
-        n = OPT["tail"]
-        for h in range(n):
-            c = slice(h * S // n, (h + 1) * S // n)
-            weave(nc.scalar.copy if h >= n - OPT["ils"] else vcopy, woven[:, c, :], res[:, :, c])
-        for h in range(n):
-            c = slice(h * S // n, (h + 1) * S // n)
-            nc.vector.quantize_mx(out=o_w[:, c].bitcast(FP8X4), scales=o_s[:, c], in_=woven[:, c, :].rearrange("p c t -> p (c t)"))
-            nc.sync.dma_start(words_of(out_1)[:, c], o_w[:, c].bitcast(I32))
+        picked_s = deal(nc.vector.tensor_copy, pick(d_s, k1_l, U8, "dk_s"), U8, "picked_s")
         for r in range(PACK):
-            nc.scalar.dma_start(out_2[0, r:16:4, :].bitcast(I32), o_s[r:P:32, :].bitcast(I32))
+            first = GROUP * (r // 2) + r % 2
+            nc.sync.dma_start(key_s[r:P:QUAD, :].bitcast(I32), picked_s[first:P:QUAD, :].bitcast(I32))
+        key_w = deal(nc.vector.tensor_copy, pick(d_w, k1_l, U32, "dk_w"), U32, "key_w")
+
+        z2_w, z2_s = quantise(z2, "z2")
+        form_st(LAST)
+        cand_w = deal(nc.vector.tensor_copy, pick(x_w, cand_l, U32, "xc_w"), U32, "cand_w")
+        cand_s = deal(nc.vector.tensor_copy, pick(x_s, cand_l, U8, "xc_s"), U8, "cand_s")
+
+        st_gate = held([P, PACK, S], F32, "st_gate", tag="scalar_out")
+        z = held([P, PACK, S], BF16, "z", tag="planes")
+        for t in PLANES:
+            nc.scalar.activation(st_gate[:, t, :], st_win[t][:].indirect(n2_l[:]), ACT.Sigmoid)
+            nc.vector.scalar_tensor_tensor(z[:, t, :], y_win[t][:, LO], gs_t[:, t:t + 1], st_gate[:, t, :],
+                                           ALU.mult, ALU.mult)
+        z_w, z_s = quantise(z, "z")
+
+        a = {t: a_win[t][:, LO] for t in PLANES}
+        b = {t: b_win[t][:, LO] for t in PLANES}
+        b_step = {t: a_win[t][:, HI] for t in PLANES}
+        gate = per_plane([P, S], "gate")
+        a_n5 = per_plane([P, S], "a_n5")
+        rest = per_plane([P, S], "rest")
+        result = held([P, PACK, S], F32, "result")
+        out_rows = out_0.rearrange("(p t) j -> p t j", t=PACK)
+        gate_bank = dict(zip(ON_SCALAR, (0, PACK)))
+        step_bank = dict(zip(ON_SCALAR, (1, 2)))
+        back_bank = dict(zip(ON_SCALAR, (3, 0)))
+
+        for t in PLANES:
+            b_bank = bank(t)
+            product(b_bank, t, key_w, key_s, z2_w, z2_s)
+            nc.scalar.copy(b[t], b_bank[:])
+            if t in ON_VECTOR:
+                nc.sync.dma_start(a[t], b[t])
+            else:
+                nc.scalar.activation(b_step[t], b_win[t][:].indirect(n6_l[:]), ACT.Copy, scale=-1.0)
+        a_banks = [bank(PACK + t) for t in PLANES]
+        for t in PLANES:
+            product(a_banks[t], t, cand_w, cand_s, z_w, z_s)
+        for t in ON_VECTOR:
+            nc.vector.tensor_tensor(b_step[t], b_win[t][:].indirect(n6_l[:]), a[t], ALU.subtract)
+            nc.scalar.activation(gate[t][:], b_step[t], ACT.Sigmoid, scale=SCORE_SCALE)
+            nc.vector.tensor_scalar(a[t], a_banks[t][:], SCORE_SCALE, None, ALU.mult)
+        for t in ON_SCALAR:
+            nc.scalar.activation(a[t], a_banks[t][:], ACT.Copy, scale=SCORE_SCALE)
+            nc.scalar.activation(a_n5[t][:], a_win[t][:].indirect(n5_l[:]), ACT.Copy, scale=-1.0)
+            b_less = turned_sum(bank(gate_bank[t]), [b[t], b_step[t]])
+            nc.scalar.activation(gate[t][:], b_less[:], ACT.Sigmoid, scale=-SCORE_SCALE)
+        for t in ON_VECTOR:
+            nc.vector.tensor_tensor(a_n5[t][:], a_win[t][:].indirect(n5_l[:]), gate[t][:], ALU.mult)
+            nc.vector.scalar_tensor_tensor(rest[t][:], gate[t][:], -1.0, a[t], ALU.add, ALU.mult)
+            nc.vector.tensor_tensor(result[:, t, :], a_n5[t][:], rest[t][:], ALU.subtract)
+            nc.sync.dma_start(out_rows[:, t, :], result[:, t, :])
+        for t in ON_SCALAR:
+            a_less = turned_sum(bank(step_bank[t]), [a[t], a_n5[t][:]])
+            nc.vector.tensor_tensor(rest[t][:], a_less[:], gate[t][:], ALU.mult)
+            pull = turned_sum(bank(back_bank[t]), [rest[t][:]])
+            nc.vector.tensor_tensor(result[:, t, :], a[t], pull[:], ALU.subtract)
+            nc.sync.dma_start(out_rows[:, t, :], result[:, t, :])
+
+        out_woven = held([P, S, PACK], BF16, "out_woven")
+        out_w = held([P, S], U32, "out_w")
+        out_s = held([P, S], U8, "out_s")
+        halves = [slice(0, S // 2), slice(S // 2, S)]
+        for copy, columns in zip((nc.vector.tensor_copy, nc.scalar.copy), halves):
+            weave(copy, out_woven[:, columns, :], result[:, :, columns])
+        for columns in halves:
+            nc.vector.quantize_mx(out=out_w[:, columns].bitcast(FP8X4), scales=out_s[:, columns],
+                                  in_=out_woven[:, columns, :].rearrange("p j t -> p (j t)"))
+            nc.sync.dma_start(words_of(out_1)[:, columns], out_w[:, columns].bitcast(I32))
+        for r in range(PACK):
+            queue = nc.scalar if r % 2 else nc.sync
+            queue.dma_start(out_2[0, r:BLOCKS:PACK, :].bitcast(I32), out_s[r:P:QUAD, :].bitcast(I32))

@@ -28,6 +28,7 @@ ON_VECTOR = range(0, PACK // 2)
 ON_SCALAR = range(PACK // 2, PACK)
 EARLY_ST = range(0, PACK - 1)
 LAST = PACK - 1
+N3_ON_SCALAR = range(0, 1)
 LO, HI = slice(0, S), slice(S, 2 * S)
 
 
@@ -153,24 +154,24 @@ def tile_picked_cdkeypullbhopdrms_none_po_kernel(
         y_copy = {t: y_early[:, t, :] if t in EARLY_ST else st_win[t][:, HI] for t in PLANES}
         for t in PLANES:
             nc.vector.memset(sq_win[t][:, HI], 0.0)
-            nc.gpsimd.memset(y_win[t][:, HI], 0.0)
+            nc.scalar.copy(y_win[t][:, HI], sq_win[t][:, HI])
         make_identity(nc, identity[:])
 
         y_banks = [bank(t) for t in PLANES]
         for t in PLANES:
             product(y_banks[t], t, wd_w, wd_s, xq_w, xq_s)
+            nc.scalar.activation(sq_win[t][:, LO], y_banks[t][:], ACT.Square)
         for t in PLANES:
             nc.scalar.copy(y_win[t][:, LO], y_banks[t][:])
-            nc.gpsimd.tensor_tensor(sq_win[t][:, LO], y_win[t][:, LO], y_win[t][:, LO], ALU.mult)
-        for t in PLANES:
             nc.sync.dma_start(y_copy[t], y_win[t][:, LO])
 
         z2 = held([P, PACK, S], BF16, "z2", tag="planes")
         root_turned = held([P, PACK, S], F32, "root_turned", tag="scalar_out")
-        for t in ON_VECTOR:
-            nc.vector.tensor_copy(sq_n3[t], sq_win[t][:].indirect(n3_l[:]))
-        for t in ON_SCALAR:
-            nc.scalar.activation(sq_n3[t], sq_win[t][:].indirect(n3_l[:]), ACT.Copy)
+        for t in PLANES:
+            if t in N3_ON_SCALAR:
+                nc.scalar.activation(sq_n3[t], sq_win[t][:].indirect(n3_l[:]), ACT.Copy)
+            else:
+                nc.vector.tensor_copy(sq_n3[t], sq_win[t][:].indirect(n3_l[:]))
         for t in PLANES:
             nc.scalar.activation(y_n4[t], y_win[t][:].indirect(n4_l[:]), ACT.Copy)
         for t in PLANES:

from contextlib import ExitStack

import concourse.mybir as mybir
from concourse.masks import make_identity

F32 = mybir.dt.float32
BF16 = mybir.dt.bfloat16
I32 = mybir.dt.int32
U32 = mybir.dt.uint32
U16 = mybir.dt.uint16
U8 = mybir.dt.uint8
FP8X4 = mybir.dt.float8_e4m3fn_x4
ACT = mybir.ActivationFunctionType
ALU = mybir.AluOpType

P = 128
PACK = 4
QUAD = 32
GROUP = 16
BLOCKS = 16
LINE = 16
T, S, G = 1024, 512, 2048
SCORE_SCALE = 0.0625
FLOPS = 3 * 2 * S * S * S

PLANES = range(PACK)
ON_VECTOR = range(0, PACK // 2)
ON_SCALAR = range(PACK // 2, PACK)
EARLY_ST = range(0, PACK - 1)
LAST = PACK - 1
N3_ON_SCALAR = range(0, 1)
LO, HI = slice(0, S), slice(S, 2 * S)


def tile_picked_cdkeypullbhopdrms_none_po_kernel(
    tc, x_words, x_scales, w1_words, w1_scales, gs, gk, d_words, d_scales,
    offs, n1, n2, n3, n4, cand, k1, n5, n6, out_0, out_1, out_2,
):
    nc = tc.nc
    with ExitStack() as ctx:
        keep = ctx.enter_context(tc.tile_pool(name="keep", bufs=1))
        psum = ctx.enter_context(tc.psum_pool(name="psum", bufs=1))

        def held(shape, dtype, name, tag=""):
            return keep.tile(shape, dtype, name=name, tag=tag, align_bytes=64)

        def per_plane(shape, name, planes=PLANES):
            return {t: held(shape, F32, "%s%d" % (name, t)) for t in planes}

        def bank(number):
            return psum.tile([P, S], F32, name="bank%d" % number)

        def words_of(dram):
            return dram[0].rearrange("p n t -> p (n t)").bitcast(I32)

        def load_list(dram, name):
            entries = held([P, S // GROUP], U16, name)
            nc.sync.dma_start(entries[:], dram)
            return entries

        def load_scale_rows(dst, dram):
            for r in range(PACK):
                nc.sync.dma_start(dst[r:P:QUAD, :].bitcast(I32), dram[0, r:BLOCKS:PACK, :].bitcast(I32))

        def pick(window, entries, dtype, name):
            picked = held([P, S], dtype, name)
            nc.vector.tensor_copy(picked[:], window[:].indirect(entries[:]))
            return picked

        def deal(copy, src, dtype, name):
            dealt = held([P, S], dtype, name)
            run = LINE // PACK if dtype == U32 else LINE
            copy(dealt[:].rearrange("p (t m i) -> p m t i", t=PACK, i=run),
                 src[:].rearrange("p (m i t) -> p m t i", t=PACK, i=run))
            return dealt

        def product(dst, t, left_words, left_scales, right_words, right_scales):
            rows = slice(t * P, (t + 1) * P)
            nc.tensor.matmul_mx(out=dst[:], lhsT=left_words[:, rows].bitcast(FP8X4), lhsT_scale=left_scales[:, rows],
                                rhs=right_words[:].bitcast(FP8X4), rhs_scale=right_scales[:], start=True, stop=True)

        def weave(copy, woven, planes):
            copy(woven.rearrange("p (c i) t -> p c t i", i=PACK), planes.rearrange("p t (c i) -> p c t i", i=PACK))

        def quantise(planes, name):
            woven = held([P, S, PACK], BF16, name + "_woven")
            weave(nc.vector.tensor_copy, woven[:], planes[:])
            words = held([P, S], U32, name + "_words")
            scales = held([P, S], U8, name + "_scales")
            nc.vector.quantize_mx(out=words[:].bitcast(FP8X4), scales=scales[:],
                                  in_=woven[:].rearrange("p j t -> p (j t)"))
            return words, scales

        x_s = held([P, T], U8, "x_s")
        w_s = held([P, S], U8, "w_s")
        d_s = held([P, G], U8, "d_s")
        key_s = held([P, S], U8, "key_s")
        x_w = held([P, T], U32, "x_w")
        w_w = held([P, S], U32, "w_w")
        d_w = held([P, G], U32, "d_w")
        gs_t = held([P, PACK], F32, "gs_t")
        gk_t = held([P, PACK], F32, "gk_t")
        nc.gpsimd.memset(x_s[:].bitcast(I32), 0)
        nc.gpsimd.memset(w_s[:].bitcast(I32), 0)
        nc.gpsimd.memset(d_s[:].bitcast(I32), 0)
        nc.vector.memset(key_s[:].bitcast(I32), 0)

        warm = held([P, 2], F32, "warm")
        nc.vector.memset(warm[:, 0:1], 1.0)
        nc.scalar.activation(warm[:, 1:2], warm[:, 0:1], ACT.Abs_reciprocal_sqrt)

        offs_l = load_list(offs, "offs_l")
        load_scale_rows(x_s, x_scales)
        nc.sync.dma_start(x_w[:].bitcast(I32), words_of(x_words))
        nc.sync.dma_start(w_w[:].bitcast(I32), words_of(w1_words))
        load_scale_rows(w_s, w1_scales)
        n4_l = load_list(n4, "n4_l")
        cand_l = load_list(cand, "cand_l")
        n3_l = load_list(n3, "n3_l")
        k1_l = load_list(k1, "k1_l")
        for e in range(2):
            nc.sync.dma_start(d_s[e:P:GROUP, :].bitcast(I32), d_scales[0, e:BLOCKS:2, :].bitcast(I32))
        nc.sync.dma_start(d_w[:].bitcast(I32), words_of(d_words))
        n1_l = load_list(n1, "n1_l")
        nc.sync.dma_start(gk_t[:], gk.rearrange("(p t) o -> p (t o)", t=PACK))
        nc.sync.dma_start(gs_t[:], gs.rearrange("(p t) o -> p (t o)", t=PACK))
        n2_l = load_list(n2, "n2_l")
        n6_l = load_list(n6, "n6_l")
        n5_l = load_list(n5, "n5_l")

        identity = held([P, P], F32, "identity")

        def turned_sum(dst, terms):
            steps = [(term, c) for term in terms for c in range(S // P)]
            for i, (term, c) in enumerate(steps):
                block = slice(c * P, (c + 1) * P)
                nc.tensor.matmul(dst[:, block], term[:, block], identity[:],
                                 start=(i == 0), stop=(i == len(steps) - 1), is_transpose=True)
            return dst

        xq_s = pick(x_s, offs_l, U8, "xq_s")
        xq_w = pick(x_w, offs_l, U32, "xq_w")
        wd_w = deal(nc.scalar.copy, w_w, U32, "wd_w")
        wd_s = deal(nc.vector.tensor_copy, w_s, U8, "wd_s")

        y_win = per_plane([P, 2 * S], "y")
        sq_win = per_plane([P, 2 * S], "sq")
        st_win = per_plane([P, 2 * S], "st")
        b_win = per_plane([P, 2 * S], "b")
        a_win = per_plane([P, 2 * S], "a")
        y_n4 = {t: b_win[t][:, HI] if t in EARLY_ST else st_win[t][:, LO] for t in PLANES}
        sq_n3 = {t: st_win[t][:, HI] if t in EARLY_ST else b_win[t][:, HI] for t in PLANES}
        y_early = held([P, len(EARLY_ST), S], F32, "y_early", tag="planes")
        y_copy = {t: y_early[:, t, :] if t in EARLY_ST else st_win[t][:, HI] for t in PLANES}
        for t in PLANES:
            nc.vector.memset(sq_win[t][:, HI], 0.0)
            nc.scalar.copy(y_win[t][:, HI], sq_win[t][:, HI])
        make_identity(nc, identity[:])

        y_banks = [bank(t) for t in PLANES]
        for t in PLANES:
            product(y_banks[t], t, wd_w, wd_s, xq_w, xq_s)
            nc.scalar.activation(sq_win[t][:, LO], y_banks[t][:], ACT.Square)
        for t in PLANES:
            nc.scalar.copy(y_win[t][:, LO], y_banks[t][:])
            nc.sync.dma_start(y_copy[t], y_win[t][:, LO])

        z2 = held([P, PACK, S], BF16, "z2", tag="planes")
        root_turned = held([P, PACK, S], F32, "root_turned", tag="scalar_out")
        for t in PLANES:
            if t in N3_ON_SCALAR:
                nc.scalar.activation(sq_n3[t], sq_win[t][:].indirect(n3_l[:]), ACT.Copy)
            else:
                nc.vector.tensor_copy(sq_n3[t], sq_win[t][:].indirect(n3_l[:]))
        for t in PLANES:
            nc.scalar.activation(y_n4[t], y_win[t][:].indirect(n4_l[:]), ACT.Copy)
        for t in PLANES:
            total = turned_sum(bank(PACK + t), [sq_win[t][:, LO], sq_n3[t]])
            nc.scalar.activation(root_turned[:, t, :], total[:], ACT.Abs_reciprocal_sqrt, bias=0.25)
        inverse_root = [turned_sum(bank(t), [root_turned[:, t, :]]) for t in PLANES]

        def form_st(t):
            nc.vector.tensor_tensor(st_win[t][:, LO], y_win[t][:].indirect(n1_l[:]), y_copy[t], ALU.subtract)

        for t in EARLY_ST:
            form_st(t)
        for t in PLANES:
            nc.vector.scalar_tensor_tensor(z2[:, t, :], y_n4[t], gk_t[:, t:t + 1], inverse_root[t][:], ALU.mult, ALU.mult)

        picked_s = deal(nc.vector.tensor_copy, pick(d_s, k1_l, U8, "dk_s"), U8, "picked_s")
        for r in range(PACK):
            first = GROUP * (r // 2) + r % 2
            nc.sync.dma_start(key_s[r:P:QUAD, :].bitcast(I32), picked_s[first:P:QUAD, :].bitcast(I32))
        key_w = deal(nc.vector.tensor_copy, pick(d_w, k1_l, U32, "dk_w"), U32, "key_w")

        z2_w, z2_s = quantise(z2, "z2")
        form_st(LAST)
        cand_w = deal(nc.vector.tensor_copy, pick(x_w, cand_l, U32, "xc_w"), U32, "cand_w")
        cand_s = deal(nc.vector.tensor_copy, pick(x_s, cand_l, U8, "xc_s"), U8, "cand_s")

        st_gate = held([P, PACK, S], F32, "st_gate", tag="scalar_out")
        z = held([P, PACK, S], BF16, "z", tag="planes")
        for t in PLANES:
            nc.scalar.activation(st_gate[:, t, :], st_win[t][:].indirect(n2_l[:]), ACT.Sigmoid)
            nc.vector.scalar_tensor_tensor(z[:, t, :], y_win[t][:, LO], gs_t[:, t:t + 1], st_gate[:, t, :],
                                           ALU.mult, ALU.mult)
        z_w, z_s = quantise(z, "z")

        a = {t: a_win[t][:, LO] for t in PLANES}
        b = {t: b_win[t][:, LO] for t in PLANES}
        b_step = {t: a_win[t][:, HI] for t in PLANES}
        gate = per_plane([P, S], "gate")
        a_n5 = per_plane([P, S], "a_n5")
        rest = per_plane([P, S], "rest")
        result = held([P, PACK, S], F32, "result")
        out_rows = out_0.rearrange("(p t) j -> p t j", t=PACK)
        gate_bank = dict(zip(ON_SCALAR, (0, PACK)))
        step_bank = dict(zip(ON_SCALAR, (1, 2)))
        back_bank = dict(zip(ON_SCALAR, (3, 0)))

        for t in PLANES:
            b_bank = bank(t)
            product(b_bank, t, key_w, key_s, z2_w, z2_s)
            nc.scalar.copy(b[t], b_bank[:])
            if t in ON_VECTOR:
                nc.sync.dma_start(a[t], b[t])
            else:
                nc.scalar.activation(b_step[t], b_win[t][:].indirect(n6_l[:]), ACT.Copy, scale=-1.0)
        a_banks = [bank(PACK + t) for t in PLANES]
        for t in PLANES:
            product(a_banks[t], t, cand_w, cand_s, z_w, z_s)
        for t in ON_VECTOR:
            nc.vector.tensor_tensor(b_step[t], b_win[t][:].indirect(n6_l[:]), a[t], ALU.subtract)
            nc.scalar.activation(gate[t][:], b_step[t], ACT.Sigmoid, scale=SCORE_SCALE)
            nc.vector.tensor_scalar(a[t], a_banks[t][:], SCORE_SCALE, None, ALU.mult)
        for t in ON_SCALAR:
            nc.scalar.activation(a[t], a_banks[t][:], ACT.Copy, scale=SCORE_SCALE)
            nc.scalar.activation(a_n5[t][:], a_win[t][:].indirect(n5_l[:]), ACT.Copy, scale=-1.0)
            b_less = turned_sum(bank(gate_bank[t]), [b[t], b_step[t]])
            nc.scalar.activation(gate[t][:], b_less[:], ACT.Sigmoid, scale=-SCORE_SCALE)
        for t in ON_VECTOR:
            nc.vector.tensor_tensor(a_n5[t][:], a_win[t][:].indirect(n5_l[:]), gate[t][:], ALU.mult)
            nc.vector.scalar_tensor_tensor(rest[t][:], gate[t][:], -1.0, a[t], ALU.add, ALU.mult)
            nc.vector.tensor_tensor(result[:, t, :], a_n5[t][:], rest[t][:], ALU.subtract)
            nc.sync.dma_start(out_rows[:, t, :], result[:, t, :])
        for t in ON_SCALAR:
            a_less = turned_sum(bank(step_bank[t]), [a[t], a_n5[t][:]])
            nc.vector.tensor_tensor(rest[t][:], a_less[:], gate[t][:], ALU.mult)
            pull = turned_sum(bank(back_bank[t]), [rest[t][:]])
            nc.vector.tensor_tensor(result[:, t, :], a[t], pull[:], ALU.subtract)
            nc.sync.dma_start(out_rows[:, t, :], result[:, t, :])

        out_woven = held([P, S, PACK], BF16, "out_woven")
        out_w = held([P, S], U32, "out_w")
        out_s = held([P, S], U8, "out_s")
        halves = [slice(0, S // 2), slice(S // 2, S)]
        for copy, columns in zip((nc.vector.tensor_copy, nc.scalar.copy), halves):
            weave(copy, out_woven[:, columns, :], result[:, :, columns])
        for columns in halves:
            nc.vector.quantize_mx(out=out_w[:, columns].bitcast(FP8X4), scales=out_s[:, columns],
                                  in_=out_woven[:, columns, :].rearrange("p j t -> p (j t)"))
            nc.sync.dma_start(words_of(out_1)[:, columns], out_w[:, columns].bitcast(I32))
        for r in range(PACK):
            queue = nc.scalar if r % 2 else nc.sync
            queue.dma_start(out_2[0, r:BLOCKS:PACK, :].bitcast(I32), out_s[r:P:QUAD, :].bitcast(I32))
